import numpy as np
import ml_dtypes


def mxq(x, axis, fmt="e4m3"):
    dtype, down = {"e4m3": (ml_dtypes.float8_e4m3fn, 7), "e5m2": (ml_dtypes.float8_e5m2, 14)}[fmt]
    v = np.moveaxis(np.asarray(x, np.float32).astype(ml_dtypes.bfloat16).astype(np.float64), axis, -1)
    blocks = v.reshape(v.shape[:-1] + (-1, 32))
    amax = np.abs(blocks).max(-1, keepdims=True)
    byte = np.maximum(np.where(amax > 0, np.frexp(amax)[1] - 1 + 127, 0) - down, 1)
    scale = np.exp2(byte - 127.0)
    codes = (blocks / scale).astype(np.float32).astype(dtype).astype(np.float64)
    return np.moveaxis((codes * scale).reshape(v.shape), -1, axis)


WIDE = False


def mx_kscale(k):
    if not WIDE:
        return np.ones(k)
    levels = np.array([10, -10, 5, -5, 0])
    if k % 512:
        return np.exp2(np.random.permutation(np.resize(levels, k // 32))).repeat(32)
    a = np.empty((k // 512, 16))
    for p in range(k // 512):
        a[p, :8] = np.random.permutation(np.resize(levels, 8))
        for g in range(8):
            far = levels[np.abs(levels - a[p, g]) >= 10]
            a[p, g + 8] = far[np.random.randint(len(far))]
    return np.exp2(a.ravel()).repeat(32)


def f64(x):
    return np.asarray(x).astype(np.float64)


def striped(idx):
    return np.tile(idx.reshape(-1, 16).T, (8, 1)).astype(np.uint16)


def unstriped(offs):
    return offs[:16].T.reshape(-1).astype(np.int64)


def pack_weight(w):
    k, n = w.shape
    w = f64(np.asarray(w, np.float32).astype(ml_dtypes.bfloat16)).reshape(k // 32, 32, n)
    amax = np.abs(w).max(1)
    byte = np.clip(np.where(amax > 0, np.frexp(amax)[1] - 1 + 127 - 7, 1), 1, 254)
    scaled = (w * np.exp2(127.0 - byte)[:, None, :]).reshape(k, n).astype(np.float32)
    words = np.ascontiguousarray(scaled.reshape(k // 512, 128, 4, n).transpose(0, 1, 3, 2)).astype(ml_dtypes.float8_e4m3fn).view(np.uint8)
    return words, np.ascontiguousarray(byte.astype(np.uint8).reshape(k // 512, 16, n))


def unpack_weight(words, scales):
    g, p, n, _ = words.shape
    vals = np.ascontiguousarray(words).view(ml_dtypes.float8_e4m3fn).astype(np.float64) * np.repeat(np.exp2(scales.astype(np.float64) - 127.0), 8, axis=1)[..., None]
    return vals.transpose(0, 1, 3, 2).reshape(g * 512, n)


K, T, S, N, H = 1024, 2048, 512, 256, 512


def setup_inputs():
    n = np.random.standard_normal
    s = mx_kscale(K)[:, None]
    u = mx_kscale(H)
    packed_xT = pack_weight(n((K, T)) * s)
    return {
        "x_words": packed_xT[0],
        "x_scales": packed_xT[1],
        "hT": (n((K, H)) / np.sqrt(K) / s).astype(np.float32),
        "spk": (np.floor(np.random.uniform(0.0, 4.0, (H, S)))).astype(np.float32),
        "unit": (np.random.uniform(0.6, 1.4, (H, 1)) * u[:, None]).astype(np.float32),
        "w1": (n((H, N)) / np.sqrt(H) / u[:, None]).astype(np.float32),
        "offs": striped(np.random.permutation(T)[:S]),
        "nb": striped(np.random.permutation(S)),
    }


def reference(x_words, x_scales, hT, spk, unit, w1, offs, nb):
    hTq = mxq(f64(hT), 0, "e4m3")
    xq = unpack_weight(x_words, x_scales)[:, unstriped(offs)]
    y = hTq.T @ xq
    rate = np.exp(1.0 * np.tanh(y))
    dev = (f64(spk) - rate) / np.sqrt(rate)
    rn = rate[:, unstriped(nb)]
    hid = f64(unit) * (dev * rn)
    return mxq(f64(w1), 0, "e4m3").T @ mxq(hid, 0, "e4m3")

@@ -1,0 +1,163 @@
+from contextlib import ExitStack
+
+import concourse.mybir as mybir
+
+K, T, S, N, H = 1024, 2048, 512, 256, 512
+FLOPS = 2 * K * H * S + 2 * H * N * S
+
+F32 = mybir.dt.float32
+BF16 = mybir.dt.bfloat16
+I32 = mybir.dt.int32
+U32 = mybir.dt.uint32
+U16 = mybir.dt.uint16
+U8 = mybir.dt.uint8
+FP8X4 = mybir.dt.float8_e4m3fn_x4
+ACT = mybir.ActivationFunctionType
+ALU = mybir.AluOpType
+
+P = 128
+PACK = 4
+K_PASS = P * PACK
+PASSES = K // K_PASS
+HALF = S // 2
+LIST_HALF = HALF // 16
+RATE_SLOT = (2, 1, 0, 3)
+M_VECTOR = 80
+
+
+def tile_picked_yplcel_res_p_kernel(tc, x_words, x_scales, hT, spk, unit, w1, offs, nb, out):
+    nc = tc.nc
+    with ExitStack() as ctx:
+        keep = ctx.enter_context(tc.tile_pool(name="keep", bufs=1))
+        psum = ctx.enter_context(tc.psum_pool(name="psum", bufs=1))
+
+        offs_t = keep.tile([P, S // 16], U16, name="offs_t")
+        nb_t = keep.tile([P, S // 16], U16, name="nb_t")
+        h_raw = [keep.tile([P, PACK, H], F32, name="h_raw%d" % o) for o in range(PASSES)]
+        x_tab = [keep.tile([P, T], U32, name="x_tab%d" % o, align_bytes=64) for o in range(PASSES)]
+        w_raw = keep.tile([P, PACK, N], F32, name="w_raw")
+        spk_t = [keep.tile([P, S], F32, name="spk%d" % t) for t in range(PACK)]
+        unit_t = keep.tile([P, PACK], F32, name="unit_t")
+        s_tab = keep.tile([P, T], U8, name="s_tab", align_bytes=64)
+
+        nc.sync.dma_start(offs_t[:], offs)
+        for o in range(PASSES):
+            nc.sync.dma_start(h_raw[o][:], hT[o * K_PASS : (o + 1) * K_PASS, :].rearrange("(p j) c -> p j c", j=PACK))
+        nc.vector.memset(s_tab[:].bitcast(I32), 0)
+        for q in range(4):
+            nc.sync.dma_start(s_tab[32 * q : 32 * q + 4 * PASSES, :].bitcast(I32), x_scales[:, 4 * q : 4 * q + 4, :].bitcast(I32))
+        for o in range(PASSES):
+            nc.sync.dma_start(x_tab[o][:].bitcast(I32), x_words[o].rearrange("p n r -> p (n r)").bitcast(I32))
+        nc.sync.dma_start(w_raw[:], w1.rearrange("(p j) c -> p j c", j=PACK))
+        nc.sync.dma_start(nb_t[:], nb)
+        spk_rows = spk.rearrange("(p t) n -> p t n", t=PACK)
+        for t in range(PACK):
+            nc.sync.dma_start(spk_t[t][:], spk_rows[:, t, :])
+
+        nc.gpsimd.dma_start(unit_t[:], unit.rearrange("(p t) o -> p (t o)", t=PACK))
+
+        h_codes = []
+        h_scales = []
+        for o in range(PASSES):
+            grouped = keep.tile([P, PACK, P, PACK], BF16, name="h_grouped%d" % o, align_bytes=64)
+            dst = grouped[:].rearrange("p t m j -> p m j t")
+            src = h_raw[o][:].rearrange("p j (m t) -> p m j t", t=PACK)
+            nc.vector.tensor_copy(dst[:, :M_VECTOR], src[:, :M_VECTOR])
+            nc.scalar.activation(dst[:, M_VECTOR:], src[:, M_VECTOR:], ACT.Copy)
+            codes = keep.tile([P, H], U32, name="h_codes%d" % o, align_bytes=64)
+            scales = keep.tile([P, H], U8, name="h_scales%d" % o, align_bytes=64)
+            nc.vector.quantize_mx(out=codes[:].bitcast(FP8X4), scales=scales[:], in_=grouped[:].rearrange("p t m j -> p (t m j)"))
+            h_codes.append(codes)
+            h_scales.append(scales)
+
+        s_pick = keep.tile([P, S], U8, name="s_pick", align_bytes=64)
+        nc.vector.tensor_copy(s_pick[:], s_tab[:].indirect(offs_t[:]))
+        x_pick = [keep.tile([P, S], U32, name="x_pick%d" % o, align_bytes=64) for o in range(PASSES)]
+        nc.vector.tensor_copy(x_pick[0][:], x_tab[0][:].indirect(offs_t[:]))
+        for half in range(2):
+            nc.vector.tensor_copy(
+                x_pick[1][:, half * HALF : (half + 1) * HALF],
+                x_tab[1][:].indirect(offs_t[:, half * LIST_HALF : (half + 1) * LIST_HALF]),
+            )
+
+        pieces = [(0, 0, HALF), (0, HALF, S)] + [(t, 0, S) for t in range(1, PACK)]
+        y = [psum.tile([P, hi - lo], F32, name="y%d" % n, tag="bank%d" % n) for n, (t, lo, hi) in enumerate(pieces)]
+        for o in range(PASSES):
+            for n, (t, lo, hi) in enumerate(pieces):
+                nc.tensor.matmul_mx(
+                    out=y[n][:],
+                    lhsT=h_codes[o][:, t * P : (t + 1) * P].bitcast(FP8X4),
+                    lhsT_scale=h_scales[o][:, t * P : (t + 1) * P],
+                    rhs=x_pick[o][:, lo:hi].bitcast(FP8X4),
+                    rhs_scale=s_pick[4 * o :, lo:hi],
+                    start=(o == 0),
+                    stop=(o == PASSES - 1),
+                )
+
+        w_grouped = keep.tile([P, N, PACK], BF16, name="w_grouped", align_bytes=64)
+        nc.vector.tensor_copy(
+            w_grouped[:].rearrange("p (c i) j -> p c j i", i=2),
+            w_raw[:].rearrange("p j (c i) -> p c j i", i=2),
+        )
+        w_codes = keep.tile([P, N], U32, name="w_codes", align_bytes=64)
+        w_scales = keep.tile([P, N], U8, name="w_scales", align_bytes=64)
+        nc.vector.quantize_mx(out=w_codes[:].bitcast(FP8X4), scales=w_scales[:], in_=w_grouped[:].rearrange("p c j -> p (c j)"))
+
+        th = keep.tile([P, PACK, S], F32, name="th")
+        rate = keep.tile([P, PACK, S], F32, name="rate")
+        resid = keep.tile([P, PACK, S], F32, name="resid")
+        other = keep.tile([P, PACK, S], F32, name="other")
+        isq = keep.tile([P, PACK, S], F32, name="isq")
+        for t in range(PACK):
+            for n, (tt, lo, hi) in enumerate(pieces):
+                if tt == t:
+                    nc.scalar.activation(th[:, t, lo:hi], y[n][:], ACT.Tanh)
+            r = rate[:, RATE_SLOT[t], :]
+            nc.scalar.activation(r, th[:, t, :], ACT.Exp)
+            if t < PACK - 1:
+                nc.gpsimd.tensor_tensor(resid[:, t, :], spk_t[t][:], r, ALU.subtract)
+            for half in range(2):
+                picked = r.indirect(nb_t[:, half * LIST_HALF : (half + 1) * LIST_HALF])
+                dst = other[:, t, half * HALF : (half + 1) * HALF]
+                if t < PACK - 1:
+                    nc.vector.tensor_copy(dst, picked)
+                else:
+                    nc.scalar.activation(dst, picked, ACT.Copy)
+        for half in range(2):
+            cols = slice(half * HALF, (half + 1) * HALF)
+            nc.scalar.activation(isq[:, :, cols], th[:, :, cols], ACT.Exp, scale=-0.5)
+        for t in range(PACK):
+            if t == PACK - 1:
+                nc.vector.tensor_tensor(resid[:, t, :], spk_t[t][:], rate[:, RATE_SLOT[t], :], ALU.subtract)
+            nc.vector.scalar_tensor_tensor(rate[:, t, :], other[:, t, :], unit_t[:, t : t + 1], resid[:, t, :], ALU.mult, ALU.mult)
+
+        for half in range(2):
+            cols = slice(half * HALF, (half + 1) * HALF)
+            hid = keep.tile([P, HALF, PACK], BF16, name="hid%d" % half, align_bytes=64)
+            nc.vector.tensor_tensor(
+                hid[:].rearrange("p (c i) t -> p c t i", i=2),
+                rate[:, :, cols].rearrange("p t (c i) -> p c t i", i=2),
+                isq[:, :, cols].rearrange("p t (c i) -> p c t i", i=2),
+                ALU.mult,
+            )
+            codes = keep.tile([P, HALF], U32, name="hid_codes%d" % half, align_bytes=64)
+            scales = keep.tile([P, HALF], U8, name="hid_scales%d" % half, align_bytes=64)
+            nc.vector.quantize_mx(out=codes[:].bitcast(FP8X4), scales=scales[:], in_=hid[:].rearrange("p c t -> p (c t)"))
+            for b in range(N // P):
+                n = (5 + 2 * half + b) % 8
+                acc = psum.tile([P, HALF], F32, name="acc%d_%d" % (half, b), tag="bank%d" % n)
+                nc.tensor.matmul_mx(
+                    out=acc[:],
+                    lhsT=w_codes[:, b * P : (b + 1) * P].bitcast(FP8X4),
+                    lhsT_scale=w_scales[:, b * P : (b + 1) * P],
+                    rhs=codes[:].bitcast(FP8X4),
+                    rhs_scale=scales[:],
+                    start=True,
+                    stop=True,
+                )
+                res = keep.tile([P, HALF], F32, name="res%d_%d" % (half, b))
+                if half == 1 and b == 1:
+                    nc.vector.tensor_copy(res[:], acc[:])
+                else:
+                    nc.scalar.copy(res[:], acc[:])
+                nc.sync.dma_start(out[b * P : (b + 1) * P, cols], res[:])

@@ -21,8 +21,8 @@ K_PASS = P * PACK
 PASSES = K // K_PASS
 HALF = S // 2
 LIST_HALF = HALF // 16
-RATE_SLOT = (2, 1, 0, 3)
 M_VECTOR = 80
+OUT_PIECES = ((0,256,),(256,384,),(384,512,),)
 
 
 def tile_picked_yplcel_res_p_kernel(tc, x_words, x_scales, hT, spk, unit, w1, offs, nb, out):
@@ -34,19 +34,15 @@ def tile_picked_yplcel_res_p_kernel(tc, x_words, x_scales, hT, spk, unit, w1, of
         offs_t = keep.tile([P, S // 16], U16, name="offs_t")
         nb_t = keep.tile([P, S // 16], U16, name="nb_t")
         h_raw = [keep.tile([P, PACK, H], F32, name="h_raw%d" % o) for o in range(PASSES)]
-        x_tab = [keep.tile([P, T], U32, name="x_tab%d" % o, align_bytes=64) for o in range(PASSES)]
+        x_tab = [keep.tile([P, T], U32, name="x_tab%d" % o, tag="x_tab%d" % o, align_bytes=64) for o in range(PASSES)]
         w_raw = keep.tile([P, PACK, N], F32, name="w_raw")
         spk_t = [keep.tile([P, S], F32, name="spk%d" % t) for t in range(PACK)]
         unit_t = keep.tile([P, PACK], F32, name="unit_t")
-        s_tab = keep.tile([P, T], U8, name="s_tab", align_bytes=64)
+        s_tab = keep.tile([P, T], U8, name="s_tab", tag="s_tab", align_bytes=64)
 
         nc.sync.dma_start(offs_t[:], offs)
         for o in range(PASSES):
             nc.sync.dma_start(h_raw[o][:], hT[o * K_PASS : (o + 1) * K_PASS, :].rearrange("(p j) c -> p j c", j=PACK))
-        nc.vector.memset(s_tab[:].bitcast(I32), 0)
-        for q in range(4):
-            nc.sync.dma_start(s_tab[32 * q : 32 * q + 4 * PASSES, :].bitcast(I32), x_scales[:, 4 * q : 4 * q + 4, :].bitcast(I32))
-        for o in range(PASSES):
             nc.sync.dma_start(x_tab[o][:].bitcast(I32), x_words[o].rearrange("p n r -> p (n r)").bitcast(I32))
         nc.sync.dma_start(w_raw[:], w1.rearrange("(p j) c -> p j c", j=PACK))
         nc.sync.dma_start(nb_t[:], nb)
@@ -54,12 +50,13 @@ def tile_picked_yplcel_res_p_kernel(tc, x_words, x_scales, hT, spk, unit, w1, of
         for t in range(PACK):
             nc.sync.dma_start(spk_t[t][:], spk_rows[:, t, :])
 
-        nc.gpsimd.dma_start(unit_t[:], unit.rearrange("(p t) o -> p (t o)", t=PACK))
+        nc.gpsimd.memset(s_tab[:].bitcast(I32), 0)
+        for q in range(4):
+            nc.gpsimd.dma_start(s_tab[32 * q : 32 * q + 4 * PASSES, :].bitcast(I32), x_scales[:, 4 * q : 4 * q + 4, :].bitcast(I32))
+        nc.sync.dma_start(unit_t[:], unit.rearrange("(p t) o -> p (t o)", t=PACK))
 
-        h_codes = []
-        h_scales = []
-        for o in range(PASSES):
-            grouped = keep.tile([P, PACK, P, PACK], BF16, name="h_grouped%d" % o, align_bytes=64)
+        def quantise_h(o):
+            grouped = keep.tile([P, PACK, P, PACK], BF16, name="h_grouped%d" % o, tag=("h_grouped0", "x_tab0")[o], align_bytes=64)
             dst = grouped[:].rearrange("p t m j -> p m j t")
             src = h_raw[o][:].rearrange("p j (m t) -> p m j t", t=PACK)
             nc.vector.tensor_copy(dst[:, :M_VECTOR], src[:, :M_VECTOR])
@@ -67,23 +64,28 @@ def tile_picked_yplcel_res_p_kernel(tc, x_words, x_scales, hT, spk, unit, w1, of
             codes = keep.tile([P, H], U32, name="h_codes%d" % o, align_bytes=64)
             scales = keep.tile([P, H], U8, name="h_scales%d" % o, align_bytes=64)
             nc.vector.quantize_mx(out=codes[:].bitcast(FP8X4), scales=scales[:], in_=grouped[:].rearrange("p t m j -> p (t m j)"))
-            h_codes.append(codes)
-            h_scales.append(scales)
+            return codes, scales
 
+        h0 = quantise_h(0)
         s_pick = keep.tile([P, S], U8, name="s_pick", align_bytes=64)
         nc.vector.tensor_copy(s_pick[:], s_tab[:].indirect(offs_t[:]))
-        x_pick = [keep.tile([P, S], U32, name="x_pick%d" % o, align_bytes=64) for o in range(PASSES)]
-        nc.vector.tensor_copy(x_pick[0][:], x_tab[0][:].indirect(offs_t[:]))
+        x_pick0 = keep.tile([P, S], U32, name="x_pick0", tag="s_tab", align_bytes=64)
+        nc.vector.tensor_copy(x_pick0[:], x_tab[0][:].indirect(offs_t[:]))
+        h1 = quantise_h(1)
+        x_pick1 = keep.tile([P, S], U32, name="x_pick1", tag="x_tab0", align_bytes=64)
         for half in range(2):
             nc.vector.tensor_copy(
-                x_pick[1][:, half * HALF : (half + 1) * HALF],
+                x_pick1[:, half * HALF : (half + 1) * HALF],
                 x_tab[1][:].indirect(offs_t[:, half * LIST_HALF : (half + 1) * LIST_HALF]),
             )
+        x_pick = [x_pick0, x_pick1]
+        h_codes = [h0[0], h1[0]]
+        h_scales = [h0[1], h1[1]]
 
         pieces = [(0, 0, HALF), (0, HALF, S)] + [(t, 0, S) for t in range(1, PACK)]
         y = [psum.tile([P, hi - lo], F32, name="y%d" % n, tag="bank%d" % n) for n, (t, lo, hi) in enumerate(pieces)]
-        for o in range(PASSES):
-            for n, (t, lo, hi) in enumerate(pieces):
+        for n, (t, lo, hi) in enumerate(pieces):
+            for o in range(PASSES):
                 nc.tensor.matmul_mx(
                     out=y[n][:],
                     lhsT=h_codes[o][:, t * P : (t + 1) * P].bitcast(FP8X4),
@@ -94,7 +96,7 @@ def tile_picked_yplcel_res_p_kernel(tc, x_words, x_scales, hT, spk, unit, w1, of
                     stop=(o == PASSES - 1),
                 )
 
-        w_grouped = keep.tile([P, N, PACK], BF16, name="w_grouped", align_bytes=64)
+        w_grouped = keep.tile([P, N, PACK], BF16, name="w_grouped", tag="x_tab1", align_bytes=64)
         nc.vector.tensor_copy(
             w_grouped[:].rearrange("p (c i) j -> p c j i", i=2),
             w_raw[:].rearrange("p j (c i) -> p c j i", i=2),
@@ -104,48 +106,57 @@ def tile_picked_yplcel_res_p_kernel(tc, x_words, x_scales, hT, spk, unit, w1, of
         nc.vector.quantize_mx(out=w_codes[:].bitcast(FP8X4), scales=w_scales[:], in_=w_grouped[:].rearrange("p c j -> p (c j)"))
 
         th = keep.tile([P, PACK, S], F32, name="th")
-        rate = keep.tile([P, PACK, S], F32, name="rate")
+        rate = [keep.tile([P, S], F32, name="rate%d" % t) for t in range(PACK)]
         resid = keep.tile([P, PACK, S], F32, name="resid")
         other = keep.tile([P, PACK, S], F32, name="other")
         isq = keep.tile([P, PACK, S], F32, name="isq")
+        prod = keep.tile([P, PACK, S], F32, name="prod")
+
+        def picked(t, half):
+            return rate[t][:].indirect(nb_t[:, half * LIST_HALF : (half + 1) * LIST_HALF])
+
+        def product(t, lo, hi):
+            nc.vector.scalar_tensor_tensor(prod[:, t, lo:hi], other[:, t, lo:hi], unit_t[:, t : t + 1], resid[:, t, lo:hi], ALU.mult, ALU.mult)
+
         for t in range(PACK):
             for n, (tt, lo, hi) in enumerate(pieces):
                 if tt == t:
                     nc.scalar.activation(th[:, t, lo:hi], y[n][:], ACT.Tanh)
-            r = rate[:, RATE_SLOT[t], :]
-            nc.scalar.activation(r, th[:, t, :], ACT.Exp)
-            if t < PACK - 1:
-                nc.gpsimd.tensor_tensor(resid[:, t, :], spk_t[t][:], r, ALU.subtract)
-            for half in range(2):
-                picked = r.indirect(nb_t[:, half * LIST_HALF : (half + 1) * LIST_HALF])
-                dst = other[:, t, half * HALF : (half + 1) * HALF]
-                if t < PACK - 1:
-                    nc.vector.tensor_copy(dst, picked)
-                else:
-                    nc.scalar.activation(dst, picked, ACT.Copy)
-        for half in range(2):
-            cols = slice(half * HALF, (half + 1) * HALF)
-            nc.scalar.activation(isq[:, :, cols], th[:, :, cols], ACT.Exp, scale=-0.5)
-        for t in range(PACK):
-            if t == PACK - 1:
-                nc.vector.tensor_tensor(resid[:, t, :], spk_t[t][:], rate[:, RATE_SLOT[t], :], ALU.subtract)
-            nc.vector.scalar_tensor_tensor(rate[:, t, :], other[:, t, :], unit_t[:, t : t + 1], resid[:, t, :], ALU.mult, ALU.mult)
+                    nc.scalar.activation(rate[t][:, lo:hi], th[:, t, lo:hi], ACT.Exp)
+        def gather(engine, t, half):
+            dst = other[:, t, half * HALF : (half + 1) * HALF]
+            if engine == "scalar":
+                nc.scalar.activation(dst, picked(t, half), ACT.Copy)
+            else:
+                nc.vector.tensor_copy(dst, picked(t, half))
 
-        for half in range(2):
-            cols = slice(half * HALF, (half + 1) * HALF)
-            hid = keep.tile([P, HALF, PACK], BF16, name="hid%d" % half, align_bytes=64)
+        def root(n):
+            lo, hi = OUT_PIECES[n]
+            nc.scalar.activation(isq[:, :, lo:hi], th[:, :, lo:hi], ACT.Exp, scale=-0.5)
+
+        def residual(t, lo=0, hi=S):
+            nc.vector.tensor_tensor(resid[:, t, lo:hi], spk_t[t][:, lo:hi], rate[t][:, lo:hi], ALU.subtract)
+
+        hid = [keep.tile([P, hi - lo, PACK], BF16, name="hid%d" % lo, align_bytes=64) for lo, hi in OUT_PIECES]
+
+        def make_hid(n):
+            lo, hi = OUT_PIECES[n]
             nc.vector.tensor_tensor(
-                hid[:].rearrange("p (c i) t -> p c t i", i=2),
-                rate[:, :, cols].rearrange("p t (c i) -> p c t i", i=2),
-                isq[:, :, cols].rearrange("p t (c i) -> p c t i", i=2),
+                hid[n][:].rearrange("p (c i) t -> p c t i", i=2),
+                prod[:, :, lo:hi].rearrange("p t (c i) -> p c t i", i=2),
+                isq[:, :, lo:hi].rearrange("p t (c i) -> p c t i", i=2),
                 ALU.mult,
             )
-            codes = keep.tile([P, HALF], U32, name="hid_codes%d" % half, align_bytes=64)
-            scales = keep.tile([P, HALF], U8, name="hid_scales%d" % half, align_bytes=64)
-            nc.vector.quantize_mx(out=codes[:].bitcast(FP8X4), scales=scales[:], in_=hid[:].rearrange("p c t -> p (c t)"))
+
+        def finish(n):
+            lo, hi = OUT_PIECES[n]
+            width = hi - lo
+            last = n == len(OUT_PIECES) - 1
+            codes = keep.tile([P, width], U32, name="hid_codes%d" % n, align_bytes=64)
+            scales = keep.tile([P, width], U8, name="hid_scales%d" % n, align_bytes=64)
+            nc.vector.quantize_mx(out=codes[:].bitcast(FP8X4), scales=scales[:], in_=hid[n][:].rearrange("p c t -> p (c t)"))
             for b in range(N // P):
-                n = (5 + 2 * half + b) % 8
-                acc = psum.tile([P, HALF], F32, name="acc%d_%d" % (half, b), tag="bank%d" % n)
+                acc = psum.tile([P, width], F32, name="acc%d_%d" % (n, b), tag="bank%d" % ((5 + 2 * n + b) % 8))
                 nc.tensor.matmul_mx(
                     out=acc[:],
                     lhsT=w_codes[:, b * P : (b + 1) * P].bitcast(FP8X4),
@@ -155,9 +166,40 @@ def tile_picked_yplcel_res_p_kernel(tc, x_words, x_scales, hT, spk, unit, w1, of
                     start=True,
                     stop=True,
                 )
-                res = keep.tile([P, HALF], F32, name="res%d_%d" % (half, b))
-                if half == 1 and b == 1:
+                res = keep.tile([P, width], F32, name="res%d_%d" % (n, b))
+                if last and b == 1:
                     nc.vector.tensor_copy(res[:], acc[:])
                 else:
                     nc.scalar.copy(res[:], acc[:])
-                nc.sync.dma_start(out[b * P : (b + 1) * P, cols], res[:])
+                queue = nc.scalar if last and b == 0 else nc.sync
+                queue.dma_start(out[b * P : (b + 1) * P, lo:hi], res[:])
+
+        residual(0, 0, HALF)
+        gather("vector", 0, 0)
+        gather("vector", 0, 1)
+        residual(0, HALF, S)
+        gather("vector", 1, 0)
+        product(0, 0, S)
+        residual(1)
+        gather("scalar", 2, 0)
+        gather("scalar", 3, 0)
+        root(0)
+        gather("scalar", 1, 1)
+        gather("scalar", 2, 1)
+        gather("scalar", 3, 1)
+        root(1)
+        root(2)
+        residual(2)
+        product(1, 0, HALF)
+        residual(3)
+        product(2, 0, HALF)
+        product(3, 0, HALF)
+        make_hid(0)
+        product(1, HALF, S)
+        finish(0)
+        product(2, HALF, S)
+        product(3, HALF, S)
+        make_hid(1)
+        make_hid(2)
+        finish(1)
+        finish(2)

@@ -40,23 +40,28 @@ def tile_picked_yplcel_res_p_kernel(tc, x_words, x_scales, hT, spk, unit, w1, of
         unit_t = keep.tile([P, PACK], F32, name="unit_t")
         s_tab = keep.tile([P, T], U8, name="s_tab", tag="s_tab", align_bytes=64)
 
+        nc.vector.memset(s_tab[:].bitcast(I32), 0)
+        h_rows = hT.rearrange("(o p j) c -> o p j c", p=P, j=PACK)
         nc.sync.dma_start(offs_t[:], offs)
-        for o in range(PASSES):
-            nc.sync.dma_start(h_raw[o][:], hT[o * K_PASS : (o + 1) * K_PASS, :].rearrange("(p j) c -> p j c", j=PACK))
-            nc.sync.dma_start(x_tab[o][:].bitcast(I32), x_words[o].rearrange("p n r -> p (n r)").bitcast(I32))
-        nc.sync.dma_start(w_raw[:], w1.rearrange("(p j) c -> p j c", j=PACK))
-        nc.sync.dma_start(nb_t[:], nb)
-        spk_rows = spk.rearrange("(p t) n -> p t n", t=PACK)
-        for t in range(PACK):
-            nc.sync.dma_start(spk_t[t][:], spk_rows[:, t, :])
-
-        nc.gpsimd.memset(s_tab[:].bitcast(I32), 0)
-        for q in range(4):
-            nc.gpsimd.dma_start(s_tab[32 * q : 32 * q + 4 * PASSES, :].bitcast(I32), x_scales[:, 4 * q : 4 * q + 4, :].bitcast(I32))
+        nc.sync.dma_start(h_raw[0][:], h_rows[0])
         nc.sync.dma_start(unit_t[:], unit.rearrange("(p t) o -> p (t o)", t=PACK))
+        nc.sync.dma_start(h_raw[1][:], h_rows[1])
+        for q in range(4):
+            nc.sync.dma_start(s_tab[32 * q : 32 * q + 4 * PASSES, :].bitcast(I32), x_scales[:, 4 * q : 4 * q + 4, :].bitcast(I32))
+        for o in range(PASSES):
+            nc.sync.dma_start(x_tab[o][:].bitcast(I32), x_words[o].rearrange("p n r -> p (n r)").bitcast(I32))
+        spk_rows = spk.rearrange("(p t) n -> p t n", t=PACK)
+        nc.sync.dma_start(spk_t[0][:], spk_rows[:, 0, :])
+        nc.sync.dma_start(w_raw[:], w1.rearrange("(p j) c -> p j c", j=PACK))
+        nc.sync.dma_start(spk_t[1][:], spk_rows[:, 1, :])
+        nc.sync.dma_start(nb_t[:], nb)
+        for t in range(2, PACK):
+            nc.sync.dma_start(spk_t[t][:], spk_rows[:, t, :])
+        minus_unit = keep.tile([P, PACK], F32, name="minus_unit")
+        nc.vector.tensor_scalar(minus_unit[:], unit_t[:], -1.0, None, ALU.mult)
 
         def quantise_h(o):
-            grouped = keep.tile([P, PACK, P, PACK], BF16, name="h_grouped%d" % o, tag=("h_grouped0", "x_tab0")[o], align_bytes=64)
+            grouped = keep.tile([P, PACK, P, PACK], BF16, name="h_grouped%d" % o, align_bytes=64)
             dst = grouped[:].rearrange("p t m j -> p m j t")
             src = h_raw[o][:].rearrange("p j (m t) -> p m j t", t=PACK)
             nc.vector.tensor_copy(dst[:, :M_VECTOR], src[:, :M_VECTOR])
@@ -67,11 +72,11 @@ def tile_picked_yplcel_res_p_kernel(tc, x_words, x_scales, hT, spk, unit, w1, of
             return codes, scales
 
         h0 = quantise_h(0)
+        h1 = quantise_h(1)
         s_pick = keep.tile([P, S], U8, name="s_pick", align_bytes=64)
         nc.vector.tensor_copy(s_pick[:], s_tab[:].indirect(offs_t[:]))
         x_pick0 = keep.tile([P, S], U32, name="x_pick0", tag="s_tab", align_bytes=64)
         nc.vector.tensor_copy(x_pick0[:], x_tab[0][:].indirect(offs_t[:]))
-        h1 = quantise_h(1)
         x_pick1 = keep.tile([P, S], U32, name="x_pick1", tag="x_tab0", align_bytes=64)
         for half in range(2):
             nc.vector.tensor_copy(
@@ -85,15 +90,16 @@ def tile_picked_yplcel_res_p_kernel(tc, x_words, x_scales, hT, spk, unit, w1, of
         pieces = [(0, 0, HALF), (0, HALF, S)] + [(t, 0, S) for t in range(1, PACK)]
         y = [psum.tile([P, hi - lo], F32, name="y%d" % n, tag="bank%d" % n) for n, (t, lo, hi) in enumerate(pieces)]
         for n, (t, lo, hi) in enumerate(pieces):
-            for o in range(PASSES):
+            order = (0, 1) if t < 2 else (1, 0)
+            for o in order:
                 nc.tensor.matmul_mx(
                     out=y[n][:],
                     lhsT=h_codes[o][:, t * P : (t + 1) * P].bitcast(FP8X4),
                     lhsT_scale=h_scales[o][:, t * P : (t + 1) * P],
                     rhs=x_pick[o][:, lo:hi].bitcast(FP8X4),
                     rhs_scale=s_pick[4 * o :, lo:hi],
-                    start=(o == 0),
-                    stop=(o == PASSES - 1),
+                    start=(o == order[0]),
+                    stop=(o == order[-1]),
                 )
 
         w_grouped = keep.tile([P, N, PACK], BF16, name="w_grouped", tag="x_tab1", align_bytes=64)
@@ -108,34 +114,40 @@ def tile_picked_yplcel_res_p_kernel(tc, x_words, x_scales, hT, spk, unit, w1, of
         th = keep.tile([P, PACK, S], F32, name="th")
         rate = [keep.tile([P, S], F32, name="rate%d" % t) for t in range(PACK)]
         resid = keep.tile([P, PACK, S], F32, name="resid")
-        other = keep.tile([P, PACK, S], F32, name="other")
+        other = keep.tile([P, S], F32, name="other")
         isq = keep.tile([P, PACK, S], F32, name="isq")
         prod = keep.tile([P, PACK, S], F32, name="prod")
+        counted = [keep.tile([P, S], F32, name="counted%d" % t) for t in range(PACK - 1)]
+        halves = [slice(0, HALF), slice(HALF, S)]
+        last = PACK - 1
 
         def picked(t, half):
             return rate[t][:].indirect(nb_t[:, half * LIST_HALF : (half + 1) * LIST_HALF])
 
-        def product(t, lo, hi):
-            nc.vector.scalar_tensor_tensor(prod[:, t, lo:hi], other[:, t, lo:hi], unit_t[:, t : t + 1], resid[:, t, lo:hi], ALU.mult, ALU.mult)
-
+        nc.scalar.activation(counted[0][:], spk_t[0][:], ACT.Copy, scale=unit_t[:, 0:1])
+        nc.vector.tensor_scalar(counted[1][:], spk_t[1][:], unit_t[:, 1:2], None, ALU.mult)
         for t in range(PACK):
             for n, (tt, lo, hi) in enumerate(pieces):
                 if tt == t:
                     nc.scalar.activation(th[:, t, lo:hi], y[n][:], ACT.Tanh)
                     nc.scalar.activation(rate[t][:, lo:hi], th[:, t, lo:hi], ACT.Exp)
-        def gather(engine, t, half):
-            dst = other[:, t, half * HALF : (half + 1) * HALF]
-            if engine == "scalar":
-                nc.scalar.activation(dst, picked(t, half), ACT.Copy)
-            else:
-                nc.vector.tensor_copy(dst, picked(t, half))
-
-        def root(n):
-            lo, hi = OUT_PIECES[n]
+            if t == 2:
+                nc.scalar.activation(counted[2][:], spk_t[2][:], ACT.Copy, scale=unit_t[:, 2:3])
+        for half in range(2):
+            nc.scalar.activation(other[:, halves[half]], picked(last, half), ACT.Copy)
+        for lo, hi in OUT_PIECES:
             nc.scalar.activation(isq[:, :, lo:hi], th[:, :, lo:hi], ACT.Exp, scale=-0.5)
 
-        def residual(t, lo=0, hi=S):
-            nc.vector.tensor_tensor(resid[:, t, lo:hi], spk_t[t][:, lo:hi], rate[t][:, lo:hi], ALU.subtract)
+        for t in range(last):
+            for cols in halves:
+                nc.vector.scalar_tensor_tensor(resid[:, t, cols], rate[t][:, cols], minus_unit[:, t : t + 1], counted[t][:, cols], ALU.mult, ALU.add)
+            for half in range(2):
+                nc.vector.tensor_tensor(prod[:, t, halves[half]], picked(t, half), resid[:, t, halves[half]], ALU.mult)
+        for cols in halves:
+            nc.vector.tensor_tensor(resid[:, last, cols], spk_t[last][:, cols], rate[last][:, cols], ALU.subtract)
+
+        def last_product(cols):
+            nc.vector.scalar_tensor_tensor(prod[:, last, cols], other[:, cols], unit_t[:, last : last + 1], resid[:, last, cols], ALU.mult, ALU.mult)
 
         hid = [keep.tile([P, hi - lo, PACK], BF16, name="hid%d" % lo, align_bytes=64) for lo, hi in OUT_PIECES]
 
@@ -151,7 +163,7 @@ def tile_picked_yplcel_res_p_kernel(tc, x_words, x_scales, hT, spk, unit, w1, of
         def finish(n):
             lo, hi = OUT_PIECES[n]
             width = hi - lo
-            last = n == len(OUT_PIECES) - 1
+            at_end = n == len(OUT_PIECES) - 1
             codes = keep.tile([P, width], U32, name="hid_codes%d" % n, align_bytes=64)
             scales = keep.tile([P, width], U8, name="hid_scales%d" % n, align_bytes=64)
             nc.vector.quantize_mx(out=codes[:].bitcast(FP8X4), scales=scales[:], in_=hid[n][:].rearrange("p c t -> p (c t)"))
@@ -167,38 +179,17 @@ def tile_picked_yplcel_res_p_kernel(tc, x_words, x_scales, hT, spk, unit, w1, of
                     stop=True,
                 )
                 res = keep.tile([P, width], F32, name="res%d_%d" % (n, b))
-                if last and b == 1:
+                if at_end and b == 1:
                     nc.vector.tensor_copy(res[:], acc[:])
                 else:
                     nc.scalar.copy(res[:], acc[:])
-                queue = nc.scalar if last and b == 0 else nc.sync
+                queue = nc.scalar if at_end and b == 0 else nc.sync
                 queue.dma_start(out[b * P : (b + 1) * P, lo:hi], res[:])
 
-        residual(0, 0, HALF)
-        gather("vector", 0, 0)
-        gather("vector", 0, 1)
-        residual(0, HALF, S)
-        gather("vector", 1, 0)
-        product(0, 0, S)
-        residual(1)
-        gather("scalar", 2, 0)
-        gather("scalar", 3, 0)
-        root(0)
-        gather("scalar", 1, 1)
-        gather("scalar", 2, 1)
-        gather("scalar", 3, 1)
-        root(1)
-        root(2)
-        residual(2)
-        product(1, 0, HALF)
-        residual(3)
-        product(2, 0, HALF)
-        product(3, 0, HALF)
+        last_product(halves[0])
         make_hid(0)
-        product(1, HALF, S)
+        last_product(halves[1])
         finish(0)
-        product(2, HALF, S)
-        product(3, HALF, S)
         make_hid(1)
         make_hid(2)
         finish(1)

@@ -17,12 +17,15 @@ ALU = mybir.AluOpType
 
 P = 128
 PACK = 4
-K_PASS = P * PACK
-PASSES = K // K_PASS
+PASSES = K // (P * PACK)
+QUADRANTS = 4
+QUADRANT = P // QUADRANTS
+SCALE_ROWS = 4
+BANKS = 8
 HALF = S // 2
 LIST_HALF = HALF // 16
-M_VECTOR = 80
-OUT_PIECES = ((0,256,),(256,384,),(384,512,),)
+LAST = PACK - 1
+OUT_PIECES = ((0, 256), (256, 384), (384, 512))
 
 
 def tile_picked_yplcel_res_p_kernel(tc, x_words, x_scales, hT, spk, unit, w1, offs, nb, out):
@@ -34,29 +37,32 @@ def tile_picked_yplcel_res_p_kernel(tc, x_words, x_scales, hT, spk, unit, w1, of
         offs_t = keep.tile([P, S // 16], U16, name="offs_t")
         nb_t = keep.tile([P, S // 16], U16, name="nb_t")
         h_raw = [keep.tile([P, PACK, H], F32, name="h_raw%d" % o) for o in range(PASSES)]
-        x_tab = [keep.tile([P, T], U32, name="x_tab%d" % o, tag="x_tab%d" % o, align_bytes=64) for o in range(PASSES)]
+        x_table = [keep.tile([P, T], U32, name="x_table%d" % o, tag="x_table%d" % o, align_bytes=64) for o in range(PASSES)]
         w_raw = keep.tile([P, PACK, N], F32, name="w_raw")
-        spk_t = [keep.tile([P, S], F32, name="spk%d" % t) for t in range(PACK)]
+        counts = [keep.tile([P, S], F32, name="counts%d" % t) for t in range(PACK)]
         unit_t = keep.tile([P, PACK], F32, name="unit_t")
-        s_tab = keep.tile([P, T], U8, name="s_tab", tag="s_tab", align_bytes=64)
+        scale_table = keep.tile([P, T], U8, name="scale_table", tag="scale_table", align_bytes=64)
 
-        nc.vector.memset(s_tab[:].bitcast(I32), 0)
+        nc.vector.memset(scale_table[:].bitcast(I32), 0)
         h_rows = hT.rearrange("(o p j) c -> o p j c", p=P, j=PACK)
         nc.sync.dma_start(offs_t[:], offs)
         nc.sync.dma_start(h_raw[0][:], h_rows[0])
         nc.sync.dma_start(unit_t[:], unit.rearrange("(p t) o -> p (t o)", t=PACK))
         nc.sync.dma_start(h_raw[1][:], h_rows[1])
-        for q in range(4):
-            nc.sync.dma_start(s_tab[32 * q : 32 * q + 4 * PASSES, :].bitcast(I32), x_scales[:, 4 * q : 4 * q + 4, :].bitcast(I32))
+        for q in range(QUADRANTS):
+            nc.sync.dma_start(
+                scale_table[QUADRANT * q : QUADRANT * q + SCALE_ROWS * PASSES, :].bitcast(I32),
+                x_scales[:, SCALE_ROWS * q : SCALE_ROWS * (q + 1), :].bitcast(I32),
+            )
         for o in range(PASSES):
-            nc.sync.dma_start(x_tab[o][:].bitcast(I32), x_words[o].rearrange("p n r -> p (n r)").bitcast(I32))
-        spk_rows = spk.rearrange("(p t) n -> p t n", t=PACK)
-        nc.sync.dma_start(spk_t[0][:], spk_rows[:, 0, :])
+            nc.sync.dma_start(x_table[o][:].bitcast(I32), x_words[o].rearrange("p n r -> p (n r)").bitcast(I32))
+        count_rows = spk.rearrange("(p t) n -> p t n", t=PACK)
+        nc.sync.dma_start(counts[0][:], count_rows[:, 0, :])
         nc.sync.dma_start(w_raw[:], w1.rearrange("(p j) c -> p j c", j=PACK))
-        nc.sync.dma_start(spk_t[1][:], spk_rows[:, 1, :])
+        nc.sync.dma_start(counts[1][:], count_rows[:, 1, :])
         nc.sync.dma_start(nb_t[:], nb)
         for t in range(2, PACK):
-            nc.sync.dma_start(spk_t[t][:], spk_rows[:, t, :])
+            nc.sync.dma_start(counts[t][:], count_rows[:, t, :])
         minus_unit = keep.tile([P, PACK], F32, name="minus_unit")
         nc.vector.tensor_scalar(minus_unit[:], unit_t[:], -1.0, None, ALU.mult)
 
@@ -64,45 +70,44 @@ def tile_picked_yplcel_res_p_kernel(tc, x_words, x_scales, hT, spk, unit, w1, of
             grouped = keep.tile([P, PACK, P, PACK], BF16, name="h_grouped%d" % o, align_bytes=64)
             dst = grouped[:].rearrange("p t m j -> p m j t")
             src = h_raw[o][:].rearrange("p j (m t) -> p m j t", t=PACK)
-            nc.vector.tensor_copy(dst[:, :M_VECTOR], src[:, :M_VECTOR])
-            nc.scalar.activation(dst[:, M_VECTOR:], src[:, M_VECTOR:], ACT.Copy)
+            nc.vector.tensor_copy(dst[:, :, :, : PACK // 2], src[:, :, :, : PACK // 2])
+            nc.scalar.activation(dst[:, :, :, PACK // 2 :], src[:, :, :, PACK // 2 :], ACT.Copy)
             codes = keep.tile([P, H], U32, name="h_codes%d" % o, align_bytes=64)
             scales = keep.tile([P, H], U8, name="h_scales%d" % o, align_bytes=64)
             nc.vector.quantize_mx(out=codes[:].bitcast(FP8X4), scales=scales[:], in_=grouped[:].rearrange("p t m j -> p (t m j)"))
             return codes, scales
 
-        h0 = quantise_h(0)
-        h1 = quantise_h(1)
-        s_pick = keep.tile([P, S], U8, name="s_pick", align_bytes=64)
-        nc.vector.tensor_copy(s_pick[:], s_tab[:].indirect(offs_t[:]))
-        x_pick0 = keep.tile([P, S], U32, name="x_pick0", tag="s_tab", align_bytes=64)
-        nc.vector.tensor_copy(x_pick0[:], x_tab[0][:].indirect(offs_t[:]))
-        x_pick1 = keep.tile([P, S], U32, name="x_pick1", tag="x_tab0", align_bytes=64)
+        h_quantised = [quantise_h(o) for o in range(PASSES)]
+
+        x_scale_pick = keep.tile([P, S], U8, name="x_scale_pick", align_bytes=64)
+        nc.vector.tensor_copy(x_scale_pick[:], scale_table[:].indirect(offs_t[:]))
+        x_pick0 = keep.tile([P, S], U32, name="x_pick0", tag="scale_table", align_bytes=64)
+        nc.vector.tensor_copy(x_pick0[:], x_table[0][:].indirect(offs_t[:]))
+        x_pick1 = keep.tile([P, S], U32, name="x_pick1", tag="x_table0", align_bytes=64)
         for half in range(2):
             nc.vector.tensor_copy(
                 x_pick1[:, half * HALF : (half + 1) * HALF],
-                x_tab[1][:].indirect(offs_t[:, half * LIST_HALF : (half + 1) * LIST_HALF]),
+                x_table[1][:].indirect(offs_t[:, half * LIST_HALF : (half + 1) * LIST_HALF]),
             )
         x_pick = [x_pick0, x_pick1]
-        h_codes = [h0[0], h1[0]]
-        h_scales = [h0[1], h1[1]]
 
-        pieces = [(0, 0, HALF), (0, HALF, S)] + [(t, 0, S) for t in range(1, PACK)]
-        y = [psum.tile([P, hi - lo], F32, name="y%d" % n, tag="bank%d" % n) for n, (t, lo, hi) in enumerate(pieces)]
-        for n, (t, lo, hi) in enumerate(pieces):
-            order = (0, 1) if t < 2 else (1, 0)
+        y_parts = [(0, 0, HALF), (0, HALF, S)] + [(t, 0, S) for t in range(1, PACK)]
+        y = [psum.tile([P, hi - lo], F32, name="y%d" % n, tag="bank%d" % n) for n, (t, lo, hi) in enumerate(y_parts)]
+        for n, (t, lo, hi) in enumerate(y_parts):
+            order = (0, 1) if t < PACK // 2 else (1, 0)
             for o in order:
+                codes, scales = h_quantised[o]
                 nc.tensor.matmul_mx(
                     out=y[n][:],
-                    lhsT=h_codes[o][:, t * P : (t + 1) * P].bitcast(FP8X4),
-                    lhsT_scale=h_scales[o][:, t * P : (t + 1) * P],
+                    lhsT=codes[:, t * P : (t + 1) * P].bitcast(FP8X4),
+                    lhsT_scale=scales[:, t * P : (t + 1) * P],
                     rhs=x_pick[o][:, lo:hi].bitcast(FP8X4),
-                    rhs_scale=s_pick[4 * o :, lo:hi],
+                    rhs_scale=x_scale_pick[SCALE_ROWS * o :, lo:hi],
                     start=(o == order[0]),
                     stop=(o == order[-1]),
                 )
 
-        w_grouped = keep.tile([P, N, PACK], BF16, name="w_grouped", tag="x_tab1", align_bytes=64)
+        w_grouped = keep.tile([P, N, PACK], BF16, name="w_grouped", tag="x_table1", align_bytes=64)
         nc.vector.tensor_copy(
             w_grouped[:].rearrange("p (c i) j -> p c j i", i=2),
             w_raw[:].rearrange("p j (c i) -> p c j i", i=2),
@@ -111,43 +116,49 @@ def tile_picked_yplcel_res_p_kernel(tc, x_words, x_scales, hT, spk, unit, w1, of
         w_scales = keep.tile([P, N], U8, name="w_scales", align_bytes=64)
         nc.vector.quantize_mx(out=w_codes[:].bitcast(FP8X4), scales=w_scales[:], in_=w_grouped[:].rearrange("p c j -> p (c j)"))
 
-        th = keep.tile([P, PACK, S], F32, name="th")
+        tanh_y = keep.tile([P, PACK, S], F32, name="tanh_y")
         rate = [keep.tile([P, S], F32, name="rate%d" % t) for t in range(PACK)]
-        resid = keep.tile([P, PACK, S], F32, name="resid")
-        other = keep.tile([P, S], F32, name="other")
-        isq = keep.tile([P, PACK, S], F32, name="isq")
-        prod = keep.tile([P, PACK, S], F32, name="prod")
-        counted = [keep.tile([P, S], F32, name="counted%d" % t) for t in range(PACK - 1)]
+        residual = keep.tile([P, PACK, S], F32, name="residual")
+        last_neighbour = keep.tile([P, S], F32, name="last_neighbour")
+        inv_root = keep.tile([P, PACK, S], F32, name="inv_root")
+        weighted = keep.tile([P, PACK, S], F32, name="weighted")
+        unit_counts = [keep.tile([P, S], F32, name="unit_counts%d" % t) for t in range(LAST)]
         halves = [slice(0, HALF), slice(HALF, S)]
-        last = PACK - 1
 
-        def picked(t, half):
+        def neighbours(t, half):
             return rate[t][:].indirect(nb_t[:, half * LIST_HALF : (half + 1) * LIST_HALF])
 
-        nc.scalar.activation(counted[0][:], spk_t[0][:], ACT.Copy, scale=unit_t[:, 0:1])
-        nc.vector.tensor_scalar(counted[1][:], spk_t[1][:], unit_t[:, 1:2], None, ALU.mult)
+        def scale_counts_on_scalar(t):
+            nc.scalar.activation(unit_counts[t][:], counts[t][:], ACT.Copy, scale=unit_t[:, t : t + 1])
+
+        scale_counts_on_scalar(0)
+        nc.vector.tensor_scalar(unit_counts[1][:], counts[1][:], unit_t[:, 1:2], None, ALU.mult)
         for t in range(PACK):
-            for n, (tt, lo, hi) in enumerate(pieces):
-                if tt == t:
-                    nc.scalar.activation(th[:, t, lo:hi], y[n][:], ACT.Tanh)
-                    nc.scalar.activation(rate[t][:, lo:hi], th[:, t, lo:hi], ACT.Exp)
-            if t == 2:
-                nc.scalar.activation(counted[2][:], spk_t[2][:], ACT.Copy, scale=unit_t[:, 2:3])
+            for n, (plane, lo, hi) in enumerate(y_parts):
+                if plane == t:
+                    nc.scalar.activation(tanh_y[:, t, lo:hi], y[n][:], ACT.Tanh)
+                    nc.scalar.activation(rate[t][:, lo:hi], tanh_y[:, t, lo:hi], ACT.Exp)
+            if t == LAST - 1:
+                scale_counts_on_scalar(t)
         for half in range(2):
-            nc.scalar.activation(other[:, halves[half]], picked(last, half), ACT.Copy)
+            nc.scalar.activation(last_neighbour[:, halves[half]], neighbours(LAST, half), ACT.Copy)
         for lo, hi in OUT_PIECES:
-            nc.scalar.activation(isq[:, :, lo:hi], th[:, :, lo:hi], ACT.Exp, scale=-0.5)
+            nc.scalar.activation(inv_root[:, :, lo:hi], tanh_y[:, :, lo:hi], ACT.Exp, scale=-0.5)
 
-        for t in range(last):
+        for t in range(LAST):
             for cols in halves:
-                nc.vector.scalar_tensor_tensor(resid[:, t, cols], rate[t][:, cols], minus_unit[:, t : t + 1], counted[t][:, cols], ALU.mult, ALU.add)
+                nc.vector.scalar_tensor_tensor(
+                    residual[:, t, cols], rate[t][:, cols], minus_unit[:, t : t + 1], unit_counts[t][:, cols], ALU.mult, ALU.add
+                )
             for half in range(2):
-                nc.vector.tensor_tensor(prod[:, t, halves[half]], picked(t, half), resid[:, t, halves[half]], ALU.mult)
+                nc.vector.tensor_tensor(weighted[:, t, halves[half]], neighbours(t, half), residual[:, t, halves[half]], ALU.mult)
         for cols in halves:
-            nc.vector.tensor_tensor(resid[:, last, cols], spk_t[last][:, cols], rate[last][:, cols], ALU.subtract)
+            nc.vector.tensor_tensor(residual[:, LAST, cols], counts[LAST][:, cols], rate[LAST][:, cols], ALU.subtract)
 
-        def last_product(cols):
-            nc.vector.scalar_tensor_tensor(prod[:, last, cols], other[:, cols], unit_t[:, last : last + 1], resid[:, last, cols], ALU.mult, ALU.mult)
+        def weigh_last_plane(cols):
+            nc.vector.scalar_tensor_tensor(
+                weighted[:, LAST, cols], last_neighbour[:, cols], unit_t[:, LAST:], residual[:, LAST, cols], ALU.mult, ALU.mult
+            )
 
         hid = [keep.tile([P, hi - lo, PACK], BF16, name="hid%d" % lo, align_bytes=64) for lo, hi in OUT_PIECES]
 
@@ -155,8 +166,8 @@ def tile_picked_yplcel_res_p_kernel(tc, x_words, x_scales, hT, spk, unit, w1, of
             lo, hi = OUT_PIECES[n]
             nc.vector.tensor_tensor(
                 hid[n][:].rearrange("p (c i) t -> p c t i", i=2),
-                prod[:, :, lo:hi].rearrange("p t (c i) -> p c t i", i=2),
-                isq[:, :, lo:hi].rearrange("p t (c i) -> p c t i", i=2),
+                weighted[:, :, lo:hi].rearrange("p t (c i) -> p c t i", i=2),
+                inv_root[:, :, lo:hi].rearrange("p t (c i) -> p c t i", i=2),
                 ALU.mult,
             )
 
@@ -168,7 +179,8 @@ def tile_picked_yplcel_res_p_kernel(tc, x_words, x_scales, hT, spk, unit, w1, of
             scales = keep.tile([P, width], U8, name="hid_scales%d" % n, align_bytes=64)
             nc.vector.quantize_mx(out=codes[:].bitcast(FP8X4), scales=scales[:], in_=hid[n][:].rearrange("p c t -> p (c t)"))
             for b in range(N // P):
-                acc = psum.tile([P, width], F32, name="acc%d_%d" % (n, b), tag="bank%d" % ((5 + 2 * n + b) % 8))
+                bank = (len(y_parts) + (N // P) * n + b) % BANKS
+                acc = psum.tile([P, width], F32, name="acc%d_%d" % (n, b), tag="bank%d" % bank)
                 nc.tensor.matmul_mx(
                     out=acc[:],
                     lhsT=w_codes[:, b * P : (b + 1) * P].bitcast(FP8X4),
@@ -186,9 +198,9 @@ def tile_picked_yplcel_res_p_kernel(tc, x_words, x_scales, hT, spk, unit, w1, of
                 queue = nc.scalar if at_end and b == 0 else nc.sync
                 queue.dma_start(out[b * P : (b + 1) * P, lo:hi], res[:])
 
-        last_product(halves[0])
+        weigh_last_plane(halves[0])
         make_hid(0)
-        last_product(halves[1])
+        weigh_last_plane(halves[1])
         finish(0)
         make_hid(1)
         make_hid(2)

from contextlib import ExitStack

import concourse.mybir as mybir

K, T, S, N, H = 1024, 2048, 512, 256, 512
FLOPS = 2 * K * H * S + 2 * H * N * S

F32 = mybir.dt.float32
BF16 = mybir.dt.bfloat16
I32 = mybir.dt.int32
U32 = mybir.dt.uint32
U16 = mybir.dt.uint16
U8 = mybir.dt.uint8
FP8X4 = mybir.dt.float8_e4m3fn_x4
ACT = mybir.ActivationFunctionType
ALU = mybir.AluOpType

P = 128
PACK = 4
PASSES = K // (P * PACK)
QUADRANTS = 4
QUADRANT = P // QUADRANTS
SCALE_ROWS = 4
BANKS = 8
HALF = S // 2
LIST_HALF = HALF // 16
LAST = PACK - 1
OUT_PIECES = ((0, 256), (256, 384), (384, 512))


def tile_picked_yplcel_res_p_kernel(tc, x_words, x_scales, hT, spk, unit, w1, offs, nb, out):
    nc = tc.nc
    with ExitStack() as ctx:
        keep = ctx.enter_context(tc.tile_pool(name="keep", bufs=1))
        psum = ctx.enter_context(tc.psum_pool(name="psum", bufs=1))

        offs_t = keep.tile([P, S // 16], U16, name="offs_t")
        nb_t = keep.tile([P, S // 16], U16, name="nb_t")
        h_raw = [keep.tile([P, PACK, H], F32, name="h_raw%d" % o) for o in range(PASSES)]
        x_table = [keep.tile([P, T], U32, name="x_table%d" % o, tag="x_table%d" % o, align_bytes=64) for o in range(PASSES)]
        w_raw = keep.tile([P, PACK, N], F32, name="w_raw")
        counts = [keep.tile([P, S], F32, name="counts%d" % t) for t in range(PACK)]
        unit_t = keep.tile([P, PACK], F32, name="unit_t")
        scale_table = keep.tile([P, T], U8, name="scale_table", tag="scale_table", align_bytes=64)

        nc.vector.memset(scale_table[:].bitcast(I32), 0)
        h_rows = hT.rearrange("(o p j) c -> o p j c", p=P, j=PACK)
        nc.sync.dma_start(offs_t[:], offs)
        nc.sync.dma_start(h_raw[0][:], h_rows[0])
        nc.sync.dma_start(unit_t[:], unit.rearrange("(p t) o -> p (t o)", t=PACK))
        nc.sync.dma_start(h_raw[1][:], h_rows[1])
        for q in range(QUADRANTS):
            nc.sync.dma_start(
                scale_table[QUADRANT * q : QUADRANT * q + SCALE_ROWS * PASSES, :].bitcast(I32),
                x_scales[:, SCALE_ROWS * q : SCALE_ROWS * (q + 1), :].bitcast(I32),
            )
        for o in range(PASSES):
            nc.sync.dma_start(x_table[o][:].bitcast(I32), x_words[o].rearrange("p n r -> p (n r)").bitcast(I32))
        count_rows = spk.rearrange("(p t) n -> p t n", t=PACK)
        nc.sync.dma_start(counts[0][:], count_rows[:, 0, :])
        nc.sync.dma_start(w_raw[:], w1.rearrange("(p j) c -> p j c", j=PACK))
        nc.sync.dma_start(counts[1][:], count_rows[:, 1, :])
        nc.sync.dma_start(nb_t[:], nb)
        for t in range(2, PACK):
            nc.sync.dma_start(counts[t][:], count_rows[:, t, :])
        minus_unit = keep.tile([P, PACK], F32, name="minus_unit")
        nc.vector.tensor_scalar(minus_unit[:], unit_t[:], -1.0, None, ALU.mult)

        def quantise_h(o):
            grouped = keep.tile([P, PACK, P, PACK], BF16, name="h_grouped%d" % o, align_bytes=64)
            dst = grouped[:].rearrange("p t m j -> p m j t")
            src = h_raw[o][:].rearrange("p j (m t) -> p m j t", t=PACK)
            nc.vector.tensor_copy(dst[:, :, :, : PACK // 2], src[:, :, :, : PACK // 2])
            nc.scalar.activation(dst[:, :, :, PACK // 2 :], src[:, :, :, PACK // 2 :], ACT.Copy)
            codes = keep.tile([P, H], U32, name="h_codes%d" % o, align_bytes=64)
            scales = keep.tile([P, H], U8, name="h_scales%d" % o, align_bytes=64)
            nc.vector.quantize_mx(out=codes[:].bitcast(FP8X4), scales=scales[:], in_=grouped[:].rearrange("p t m j -> p (t m j)"))
            return codes, scales

        h_quantised = [quantise_h(o) for o in range(PASSES)]

        x_scale_pick = keep.tile([P, S], U8, name="x_scale_pick", align_bytes=64)
        nc.vector.tensor_copy(x_scale_pick[:], scale_table[:].indirect(offs_t[:]))
        x_pick0 = keep.tile([P, S], U32, name="x_pick0", tag="scale_table", align_bytes=64)
        nc.vector.tensor_copy(x_pick0[:], x_table[0][:].indirect(offs_t[:]))
        x_pick1 = keep.tile([P, S], U32, name="x_pick1", tag="x_table0", align_bytes=64)
        for half in range(2):
            nc.vector.tensor_copy(
                x_pick1[:, half * HALF : (half + 1) * HALF],
                x_table[1][:].indirect(offs_t[:, half * LIST_HALF : (half + 1) * LIST_HALF]),
            )
        x_pick = [x_pick0, x_pick1]

        y_parts = [(0, 0, HALF), (0, HALF, S)] + [(t, 0, S) for t in range(1, PACK)]
        y = [psum.tile([P, hi - lo], F32, name="y%d" % n, tag="bank%d" % n) for n, (t, lo, hi) in enumerate(y_parts)]
        for n, (t, lo, hi) in enumerate(y_parts):
            order = (0, 1) if t < PACK // 2 else (1, 0)
            for o in order:
                codes, scales = h_quantised[o]
                nc.tensor.matmul_mx(
                    out=y[n][:],
                    lhsT=codes[:, t * P : (t + 1) * P].bitcast(FP8X4),
                    lhsT_scale=scales[:, t * P : (t + 1) * P],
                    rhs=x_pick[o][:, lo:hi].bitcast(FP8X4),
                    rhs_scale=x_scale_pick[SCALE_ROWS * o :, lo:hi],
                    start=(o == order[0]),
                    stop=(o == order[-1]),
                )

        w_grouped = keep.tile([P, N, PACK], BF16, name="w_grouped", tag="x_table1", align_bytes=64)
        nc.vector.tensor_copy(
            w_grouped[:].rearrange("p (c i) j -> p c j i", i=2),
            w_raw[:].rearrange("p j (c i) -> p c j i", i=2),
        )
        w_codes = keep.tile([P, N], U32, name="w_codes", align_bytes=64)
        w_scales = keep.tile([P, N], U8, name="w_scales", align_bytes=64)
        nc.vector.quantize_mx(out=w_codes[:].bitcast(FP8X4), scales=w_scales[:], in_=w_grouped[:].rearrange("p c j -> p (c j)"))

        tanh_y = keep.tile([P, PACK, S], F32, name="tanh_y")
        rate = [keep.tile([P, S], F32, name="rate%d" % t) for t in range(PACK)]
        residual = keep.tile([P, PACK, S], F32, name="residual")
        last_neighbour = keep.tile([P, S], F32, name="last_neighbour")
        inv_root = keep.tile([P, PACK, S], F32, name="inv_root")
        weighted = keep.tile([P, PACK, S], F32, name="weighted")
        unit_counts = [keep.tile([P, S], F32, name="unit_counts%d" % t) for t in range(LAST)]
        halves = [slice(0, HALF), slice(HALF, S)]

        def neighbours(t, half):
            return rate[t][:].indirect(nb_t[:, half * LIST_HALF : (half + 1) * LIST_HALF])

        def scale_counts_on_scalar(t):
            nc.scalar.activation(unit_counts[t][:], counts[t][:], ACT.Copy, scale=unit_t[:, t : t + 1])

        scale_counts_on_scalar(0)
        nc.vector.tensor_scalar(unit_counts[1][:], counts[1][:], unit_t[:, 1:2], None, ALU.mult)
        for t in range(PACK):
            for n, (plane, lo, hi) in enumerate(y_parts):
                if plane == t:
                    nc.scalar.activation(tanh_y[:, t, lo:hi], y[n][:], ACT.Tanh)
                    nc.scalar.activation(rate[t][:, lo:hi], tanh_y[:, t, lo:hi], ACT.Exp)
            if t == LAST - 1:
                scale_counts_on_scalar(t)
        for half in range(2):
            nc.scalar.activation(last_neighbour[:, halves[half]], neighbours(LAST, half), ACT.Copy)
        for lo, hi in OUT_PIECES:
            nc.scalar.activation(inv_root[:, :, lo:hi], tanh_y[:, :, lo:hi], ACT.Exp, scale=-0.5)

        for t in range(LAST):
            for cols in halves:
                nc.vector.scalar_tensor_tensor(
                    residual[:, t, cols], rate[t][:, cols], minus_unit[:, t : t + 1], unit_counts[t][:, cols], ALU.mult, ALU.add
                )
            for half in range(2):
                nc.vector.tensor_tensor(weighted[:, t, halves[half]], neighbours(t, half), residual[:, t, halves[half]], ALU.mult)
        for cols in halves:
            nc.vector.tensor_tensor(residual[:, LAST, cols], counts[LAST][:, cols], rate[LAST][:, cols], ALU.subtract)

        def weigh_last_plane(cols):
            nc.vector.scalar_tensor_tensor(
                weighted[:, LAST, cols], last_neighbour[:, cols], unit_t[:, LAST:], residual[:, LAST, cols], ALU.mult, ALU.mult
            )

        hid = [keep.tile([P, hi - lo, PACK], BF16, name="hid%d" % lo, align_bytes=64) for lo, hi in OUT_PIECES]

        def make_hid(n):
            lo, hi = OUT_PIECES[n]
            nc.vector.tensor_tensor(
                hid[n][:].rearrange("p (c i) t -> p c t i", i=2),
                weighted[:, :, lo:hi].rearrange("p t (c i) -> p c t i", i=2),
                inv_root[:, :, lo:hi].rearrange("p t (c i) -> p c t i", i=2),
                ALU.mult,
            )

        def finish(n):
            lo, hi = OUT_PIECES[n]
            width = hi - lo
            at_end = n == len(OUT_PIECES) - 1
            codes = keep.tile([P, width], U32, name="hid_codes%d" % n, align_bytes=64)
            scales = keep.tile([P, width], U8, name="hid_scales%d" % n, align_bytes=64)
            nc.vector.quantize_mx(out=codes[:].bitcast(FP8X4), scales=scales[:], in_=hid[n][:].rearrange("p c t -> p (c t)"))
            for b in range(N // P):
                bank = (len(y_parts) + (N // P) * n + b) % BANKS
                acc = psum.tile([P, width], F32, name="acc%d_%d" % (n, b), tag="bank%d" % bank)
                nc.tensor.matmul_mx(
                    out=acc[:],
                    lhsT=w_codes[:, b * P : (b + 1) * P].bitcast(FP8X4),
                    lhsT_scale=w_scales[:, b * P : (b + 1) * P],
                    rhs=codes[:].bitcast(FP8X4),
                    rhs_scale=scales[:],
                    start=True,
                    stop=True,
                )
                res = keep.tile([P, width], F32, name="res%d_%d" % (n, b))
                if at_end and b == 1:
                    nc.vector.tensor_copy(res[:], acc[:])
                else:
                    nc.scalar.copy(res[:], acc[:])
                queue = nc.scalar if at_end and b == 0 else nc.sync
                queue.dma_start(out[b * P : (b + 1) * P, lo:hi], res[:])

        weigh_last_plane(halves[0])
        make_hid(0)
        weigh_last_plane(halves[1])
        finish(0)
        make_hid(1)
        make_hid(2)
        finish(1)
        finish(2)
